import numpy as np
import ml_dtypes


def mxq(x, axis, fmt="e4m3"):
    dtype, down = {"e4m3": (ml_dtypes.float8_e4m3fn, 7), "e5m2": (ml_dtypes.float8_e5m2, 14)}[fmt]
    v = np.moveaxis(np.asarray(x, np.float32).astype(ml_dtypes.bfloat16).astype(np.float64), axis, -1)
    blocks = v.reshape(v.shape[:-1] + (-1, 32))
    amax = np.abs(blocks).max(-1, keepdims=True)
    byte = np.maximum(np.where(amax > 0, np.frexp(amax)[1] - 1 + 127, 0) - down, 1)
    scale = np.exp2(byte - 127.0)
    codes = (blocks / scale).astype(np.float32).astype(dtype).astype(np.float64)
    return np.moveaxis((codes * scale).reshape(v.shape), -1, axis)


WIDE = False


def mx_kscale(k):
    if not WIDE:
        return np.ones(k)
    levels = np.array([10, -10, 5, -5, 0])
    if k % 512:
        return np.exp2(np.random.permutation(np.resize(levels, k // 32))).repeat(32)
    a = np.empty((k // 512, 16))
    for p in range(k // 512):
        a[p, :8] = np.random.permutation(np.resize(levels, 8))
        for g in range(8):
            far = levels[np.abs(levels - a[p, g]) >= 10]
            a[p, g + 8] = far[np.random.randint(len(far))]
    return np.exp2(a.ravel()).repeat(32)


def f64(x):
    return np.asarray(x).astype(np.float64)


def striped(idx):
    return np.tile(idx.reshape(-1, 16).T, (8, 1)).astype(np.uint16)


def unstriped(offs):
    return offs[:16].T.reshape(-1).astype(np.int64)


def striped8(idx):
    return np.concatenate([x.reshape(-1, 16).T for x in idx]).astype(np.uint16)


def runs(offs, k):
    lists = np.stack([offs[16 * r : 16 * r + 16].T.reshape(-1) for r in range(8)]).astype(np.int64)
    return lists[np.arange(k) % 512 // 64]


def pack_weight(w):
    k, n = w.shape
    w = f64(np.asarray(w, np.float32).astype(ml_dtypes.bfloat16)).reshape(k // 32, 32, n)
    amax = np.abs(w).max(1)
    byte = np.clip(np.where(amax > 0, np.frexp(amax)[1] - 1 + 127 - 7, 1), 1, 254)
    scaled = (w * np.exp2(127.0 - byte)[:, None, :]).reshape(k, n).astype(np.float32)
    words = np.ascontiguousarray(scaled.reshape(k // 512, 128, 4, n).transpose(0, 1, 3, 2)).astype(ml_dtypes.float8_e4m3fn).view(np.uint8)
    return words, np.ascontiguousarray(byte.astype(np.uint8).reshape(k // 512, 16, n))


def unpack_weight(words, scales):
    g, p, n, _ = words.shape
    vals = np.ascontiguousarray(words).view(ml_dtypes.float8_e4m3fn).astype(np.float64) * np.repeat(np.exp2(scales.astype(np.float64) - 127.0), 8, axis=1)[..., None]
    return vals.transpose(0, 1, 3, 2).reshape(g * 512, n)


K, T, S, H, W, G = 512, 1024, 512, 512, 256, 2048


def setup_inputs():
    n = np.random.standard_normal
    s = mx_kscale(K)[:, None]
    packed_xT = pack_weight(n((K, T)) * s)
    packed_dT = pack_weight(n((K, G)) / s)
    perm = np.stack([np.random.permutation(S) for _ in range(8)])
    return {
        "x_words": packed_xT[0],
        "x_scales": packed_xT[1],
        "w1": (n((K, H)) / np.sqrt(2 * K) / s).astype(np.float32),
        "w2": (n((K, H)) / np.sqrt(2 * K) / s).astype(np.float32),
        "gs": (np.random.uniform(0.5, 1.5, (K, 1)) * s).astype(np.float32),
        "d_words": packed_dT[0],
        "d_scales": packed_dT[1],
        "offs": striped(np.random.permutation(T)[:S]),
        "hz": striped8(np.random.randint(0, T, (8, S))),
        "n1": striped8(perm[:, :W]),
        "n2": striped8(perm[:, W:]),
        "k1": striped8(np.random.randint(0, G, (8, H))),
        "n3": striped8(np.stack([np.random.permutation(S) for _ in range(8)])),
        "n4": striped8(np.stack([np.random.permutation(S) for _ in range(8)])),
    }


def reference(x_words, x_scales, w1, w2, gs, d_words, d_scales, offs, hz, n1, n2, k1, n3, n4):
    d_k1 = unpack_weight(d_words, d_scales)[np.arange(K)[:, None], runs(k1, K)]
    xq = unpack_weight(x_words, x_scales)[:, unstriped(offs)]
    x_hz = unpack_weight(x_words, x_scales)[np.arange(K)[:, None], runs(hz, K)]
    y = mxq(f64(w1), 0, "e4m3").T @ xq + mxq(f64(w2), 0, "e4m3").T @ x_hz
    pa = y[np.arange(H)[:, None], runs(n1, H)]
    pb = y[np.arange(H)[:, None], runs(n2, H)]
    rb = np.maximum(pa, pb)
    ra = pa / (np.abs(pb) + 0.5)
    ds = np.zeros((H, S))
    ds[np.arange(H)[:, None], runs(n1, H)] = ra
    dt = ds.copy()
    dt[np.arange(H)[:, None], runs(n2, H)] = rb
    z = f64(gs) * dt
    h = 0.0625 * ((d_k1.T @ mxq(z, 0, "e4m3")))
    ds2 = np.zeros((H, S))
    ds2[np.arange(H)[:, None], runs(n3, H)] = h
    return np.maximum(h, ds2[np.arange(H)[:, None], runs(n4, H)])

@@ -1,0 +1,237 @@
+from contextlib import ExitStack
+
+import concourse.mybir as mybir
+
+K, T, S, H, W, G = 512, 1024, 512, 512, 256, 2048
+FLOPS = 3 * 2 * K * H * S
+
+F32 = mybir.dt.float32
+BF16 = mybir.dt.bfloat16
+I32 = mybir.dt.int32
+U32 = mybir.dt.uint32
+U16 = mybir.dt.uint16
+U8 = mybir.dt.uint8
+FP8X4 = mybir.dt.float8_e4m3fn_x4
+ACT = mybir.ActivationFunctionType
+ALU = mybir.AluOpType
+
+P = 128
+PACK = 4
+HALF = 256
+Z_CHUNKS = ((0, 128), (128, 256), (256, 512))
+
+
+def tile_picked_thqratiorelay_none_p_kernel(
+    tc, x_words, x_scales, w1, w2, gs, d_words, d_scales, offs, hz, n1, n2, k1, n3, n4, out
+):
+    nc = tc.nc
+    with ExitStack() as ctx:
+        lists = ctx.enter_context(tc.tile_pool(name="lists", bufs=1))
+        keep = ctx.enter_context(tc.tile_pool(name="keep", bufs=1))
+        psum = ctx.enter_context(tc.psum_pool(name="psum", bufs=1))
+
+        def load_list(src, name):
+            t = lists.tile(list(src.shape), U16, name=name)
+            nc.sync.dma_start(t[:], src)
+            return t
+
+        def load_scales(queue, src, cols, name):
+            t = keep.tile([P, cols], U8, name=name, align_bytes=64)
+            rows = src[0].bitcast(I32)
+            queue.dma_start(
+                t[:].bitcast(I32), rows.unsqueeze(1).to_broadcast([16, 8, cols // 4])
+            )
+            return t
+
+        def load_words(src, cols, name, tag=None):
+            t = keep.tile([P, cols], I32, name=name, tag=tag or name, align_bytes=64)
+            nc.sync.dma_start(t[:], src[0].rearrange("p c r -> p (c r)").bitcast(I32))
+            return t
+
+        def load_weight_half(src, half, name):
+            t = keep.tile([P, PACK, HALF], F32, name=name, align_bytes=64)
+            cols = slice(half * HALF, (half + 1) * HALF)
+            nc.sync.dma_start(t[:], src.rearrange("(p j) c -> p j c", j=PACK)[:, :, cols])
+            return t
+
+        offs_t = load_list(offs, "offs_t")
+        hz_t = load_list(hz, "hz_t")
+        xs_win = load_scales(nc.sync, x_scales, T, "xs_win")
+        w_raw = {(0, 0): load_weight_half(w1, 0, "w_raw00")}
+        xw_win = load_words(x_words, T, "xw_win")
+        k1_t = load_list(k1, "k1_t")
+        n2_t = load_list(n2, "n2_t")
+        n1_t = load_list(n1, "n1_t")
+        w_raw[0, 1] = load_weight_half(w1, 1, "w_raw01")
+        w_raw[1, 0] = load_weight_half(w2, 0, "w_raw10")
+        w_raw[1, 1] = load_weight_half(w2, 1, "w_raw11")
+        n3_t = load_list(n3, "n3_t")
+        n4_t = load_list(n4, "n4_t")
+        ds_win = load_scales(nc.gpsimd, d_scales, G, "ds_win")
+        gs_t = keep.tile([P, PACK], F32, name="gs_t")
+        nc.gpsimd.dma_start(gs_t[:], gs.rearrange("(p t) o -> p (t o)", t=PACK))
+
+        x_plane = keep.tile([P, 2 * S], U8, name="x_plane", align_bytes=64)
+        d_plane = keep.tile([P, H], U8, name="d_plane", align_bytes=64)
+        nc.vector.memset(x_plane[:].bitcast(I32), 0)
+        nc.vector.memset(d_plane[:].bitcast(I32), 0)
+
+        def place_rows(queue, plane, picked):
+            for j in range(4):
+                queue.dma_start(
+                    plane[j:P:32, :].bitcast(I32), picked[8 * j : P : 32, :].bitcast(I32)
+                )
+
+        xs_picked = keep.tile([P, 2 * S], U8, name="xs_picked", align_bytes=64)
+        nc.vector.tensor_copy(xs_picked[:, :S], xs_win[:].indirect(offs_t[:]))
+        nc.vector.tensor_copy(xs_picked[:, S:], xs_win[:].indirect(hz_t[:]))
+        place_rows(nc.sync, x_plane, xs_picked)
+        xw_picked = []
+        for i, lst in enumerate((offs_t, hz_t)):
+            t = keep.tile([P, S], U32, name="xw_picked%d" % i, align_bytes=64)
+            nc.vector.tensor_copy(t[:], xw_win[:].bitcast(U32).indirect(lst[:]))
+            xw_picked.append(t)
+
+        w_codes, w_scales = [], []
+        for i in range(2):
+            grouped = keep.tile([P, PACK, P, PACK], BF16, name="w_grouped%d" % i, align_bytes=64)
+            for half in range(2):
+                dst = grouped[:, :, half * 64 : (half + 1) * 64, :].rearrange("p t m j -> p m j t")
+                src = w_raw[i, half][:].rearrange("p j (m t) -> p m j t", t=PACK)
+                if (i, half) == (1, 1):
+                    nc.vector.tensor_copy(dst, src)
+                else:
+                    nc.scalar.copy(dst, src)
+            codes = keep.tile([P, H], U32, name="w_codes%d" % i, align_bytes=64)
+            scales = keep.tile([P, H], U8, name="w_scales%d" % i, align_bytes=64)
+            flat = grouped[:].rearrange("p t m j -> p (t m j)")
+            for lo, hi in ((0, H),) if i == 0 else ((0, P), (P, H)):
+                nc.vector.quantize_mx(
+                    out=codes[:, lo:hi].bitcast(FP8X4),
+                    scales=scales[:, lo:hi],
+                    in_=flat[:, lo * PACK : hi * PACK],
+                )
+            w_codes.append(codes)
+            w_scales.append(scales)
+
+        y_banks = []
+        for t in range(PACK):
+            bank = psum.tile([P, S], F32, name="bank%d" % t)
+            cols = slice(t * P, (t + 1) * P)
+            for i in (1, 0):
+                nc.tensor.matmul_mx(
+                    out=bank[:],
+                    lhsT=w_codes[i][:, cols].bitcast(FP8X4),
+                    lhsT_scale=w_scales[i][:, cols],
+                    rhs=xw_picked[i][:].bitcast(FP8X4),
+                    rhs_scale=x_plane[:, i * S : (i + 1) * S],
+                    start=(i == 1),
+                    stop=(i == 0),
+                )
+            y_banks.append(bank)
+
+        ds_picked = keep.tile([P, H], U8, name="ds_picked", tag="w_grouped1", align_bytes=64)
+        nc.vector.tensor_copy(ds_picked[:], ds_win[:].indirect(k1_t[:]))
+        ds_dealt = keep.tile([P, H], U8, name="ds_dealt", align_bytes=64)
+        nc.vector.tensor_copy(
+            ds_dealt[:].rearrange("p (t m) -> p m t", t=PACK),
+            ds_picked[:].rearrange("p (m t) -> p m t", t=PACK),
+        )
+        place_rows(nc.sync, d_plane, ds_dealt)
+
+        dw_win = load_words(d_words, G, "dw_win", tag="w_raw00")
+        dw_picked = keep.tile([P, H], U32, name="dw_picked", align_bytes=64)
+        nc.vector.tensor_copy(dw_picked[:], dw_win[:].bitcast(U32).indirect(k1_t[:]))
+        dw_dealt = keep.tile([P, H], U32, name="dw_dealt", align_bytes=64)
+        nc.vector.tensor_copy(
+            dw_dealt[:].rearrange("p (t m) -> p m t", t=PACK),
+            dw_picked[:].rearrange("p (m t) -> p m t", t=PACK),
+        )
+
+        def weigh_and_round(t, dt_t):
+            for c, (lo, hi) in enumerate(Z_CHUNKS):
+                src = dt_t[:, lo:hi]
+                if c == 0 and t >= 2:
+                    nc.vector.tensor_scalar(
+                        z_grouped[c][:, :, t], src, gs_t[:, t : t + 1], None, ALU.mult
+                    )
+                else:
+                    nc.scalar.activation(
+                        z_grouped[c][:, :, t], src, ACT.Copy, scale=gs_t[:, t : t + 1]
+                    )
+
+        dts = []
+        for t in range(PACK):
+            y_t = keep.tile([P, S], F32, name="y%d" % t, align_bytes=64)
+            nc.scalar.copy(y_t[:], y_banks[t][:])
+            pa = keep.tile([P, W], F32, name="pa%d" % t)
+            pb = keep.tile([P, W], F32, name="pb%d" % t)
+            nc.scalar.activation(pb[:], y_t[:].indirect(n2_t[:]), ACT.Copy)
+            nc.scalar.activation(pa[:], y_t[:].indirect(n1_t[:]), ACT.Copy)
+            rb = keep.tile([P, W], F32, name="rb%d" % t)
+            nc.vector.tensor_tensor(rb[:], pa[:], pb[:], ALU.max)
+            dt_t = keep.tile([P, S], F32, name="dt%d" % t)
+            nc.vector.tensor_copy(dt_t[:].indirect(n2_t[:]), rb[:])
+            size = keep.tile([P, W], F32, name="size%d" % t, align_bytes=64)
+            nc.scalar.activation(size[:], pb[:], ACT.Abs)
+            root = keep.tile([P, W], F32, name="root%d" % t, align_bytes=64)
+            nc.scalar.activation(root[:], size[:], ACT.Abs_reciprocal_sqrt, bias=0.5)
+            inv = keep.tile([P, W], F32, name="inv%d" % t)
+            nc.scalar.activation(inv[:], root[:], ACT.Square)
+            nc.vector.tensor_tensor(dt_t[:].indirect(n1_t[:]), pa[:], inv[:], ALU.mult)
+            dts.append(dt_t)
+        z_grouped = [
+            keep.tile([P, hi - lo, PACK], BF16, name="z_grouped%d" % lo, tag=tag + str(PACK - 2), align_bytes=64)
+            for (lo, hi), tag in zip(Z_CHUNKS, ("y", "size", "root"))
+        ]
+        for t in range(PACK):
+            weigh_and_round(t, dts[t])
+
+        z_codes = keep.tile([P, S], U32, name="z_codes", align_bytes=64)
+        z_scales = keep.tile([P, S], U8, name="z_scales", align_bytes=64)
+        for c, (lo, hi) in enumerate(Z_CHUNKS):
+            nc.vector.quantize_mx(
+                out=z_codes[:, lo:hi].bitcast(FP8X4),
+                scales=z_scales[:, lo:hi],
+                in_=z_grouped[c][:].rearrange("p n t -> p (n t)"),
+            )
+
+        hs = [keep.tile([P, S], F32, name="h%d" % t) for t in range(PACK)]
+        sent = [keep.tile([P, S], F32, name="sent%d" % t) for t in range(PACK)]
+        out_rows = out.rearrange("(p t) n -> t p n", t=PACK)
+
+        def product_and_send(step, t, lo, hi):
+            bank = psum.tile([P, S], F32, name="bank%d" % ((step + PACK) % 8))
+            cols = slice(t * P, (t + 1) * P)
+            nc.tensor.matmul_mx(
+                out=bank[:, : hi - lo],
+                lhsT=dw_dealt[:, cols].bitcast(FP8X4),
+                lhsT_scale=d_plane[:, cols],
+                rhs=z_codes[:, lo:hi].bitcast(FP8X4),
+                rhs_scale=z_scales[:, lo:hi],
+                start=True,
+                stop=True,
+            )
+            part = hs[t][:, lo:hi]
+            if step == 0:
+                nc.vector.tensor_scalar(part, bank[:, : hi - lo], 0.0625, None, ALU.mult)
+            else:
+                nc.scalar.activation(part, bank[:, : hi - lo], ACT.Copy, scale=0.0625)
+            nc.vector.tensor_copy(sent[t][:].indirect(n3_t[:, lo // 16 : hi // 16]), part)
+
+        def fetch_and_store(t):
+            for c in range(2):
+                cols = slice(c * HALF, (c + 1) * HALF)
+                back = keep.tile([P, HALF], F32, name="back%d%d" % (t, c))
+                looked_up = sent[t][:].indirect(n4_t[:, c * 16 : (c + 1) * 16])
+                nc.scalar.activation(back[:], looked_up, ACT.Copy)
+                res = keep.tile([P, HALF], F32, name="res%d%d" % (t, c))
+                nc.vector.tensor_tensor(res[:], hs[t][:, cols], back[:], ALU.max)
+                nc.sync.dma_start(out_rows[t][:, cols], res[:])
+
+        order = [(0, 0, 128), (1, 0, 128), (0, 128, 256), (1, 128, 256), (0, 256, 512), (2, 0, 256), (1, 256, 512), (3, 0, 256), (2, 256, 512), (3, 256, 512)]
+        for step, (t, lo, hi) in enumerate(order):
+            product_and_send(step, t, lo, hi)
+            if step >= 1 and order[step - 1][2] == S:
+                fetch_and_store(order[step - 1][0])
+        fetch_and_store(PACK - 1)

@@ -18,6 +18,7 @@ ALU = mybir.AluOpType
 P = 128
 PACK = 4
 HALF = 256
+HELD = ("pa", "size")
 Z_CHUNKS = ((0, 128), (128, 256), (256, 512))
 
 
@@ -28,6 +29,7 @@ def tile_picked_thqratiorelay_none_p_kernel(
     with ExitStack() as ctx:
         lists = ctx.enter_context(tc.tile_pool(name="lists", bufs=1))
         keep = ctx.enter_context(tc.tile_pool(name="keep", bufs=1))
+        shared = ctx.enter_context(tc.tile_pool(name="shared", bufs=1))
         psum = ctx.enter_context(tc.psum_pool(name="psum", bufs=1))
 
         def load_list(src, name):
@@ -35,41 +37,37 @@ def tile_picked_thqratiorelay_none_p_kernel(
             nc.sync.dma_start(t[:], src)
             return t
 
-        def load_scales(queue, src, cols, name):
-            t = keep.tile([P, cols], U8, name=name, align_bytes=64)
-            rows = src[0].bitcast(I32)
-            queue.dma_start(
-                t[:].bitcast(I32), rows.unsqueeze(1).to_broadcast([16, 8, cols // 4])
-            )
-            return t
-
-        def load_words(src, cols, name, tag=None):
-            t = keep.tile([P, cols], I32, name=name, tag=tag or name, align_bytes=64)
+        def load_words(src, cols, name, pool, **place):
+            t = pool.tile([P, cols], I32, name=name, align_bytes=64, **place)
             nc.sync.dma_start(t[:], src[0].rearrange("p c r -> p (c r)").bitcast(I32))
             return t
 
-        def load_weight_half(src, half, name):
-            t = keep.tile([P, PACK, HALF], F32, name=name, align_bytes=64)
+        def load_weight_half(src, half, name, pool, **place):
+            t = pool.tile([P, PACK, HALF], F32, name=name, align_bytes=64, **place)
             cols = slice(half * HALF, (half + 1) * HALF)
             nc.sync.dma_start(t[:], src.rearrange("(p j) c -> p j c", j=PACK)[:, :, cols])
             return t
 
         offs_t = load_list(offs, "offs_t")
         hz_t = load_list(hz, "hz_t")
-        xs_win = load_scales(nc.sync, x_scales, T, "xs_win")
-        w_raw = {(0, 0): load_weight_half(w1, 0, "w_raw00")}
-        xw_win = load_words(x_words, T, "xw_win")
+        xs_win = keep.tile([P, T], U8, name="xs_win", align_bytes=64)
+        nc.sync.dma_start(
+            xs_win[:].bitcast(I32),
+            x_scales[0].bitcast(I32).unsqueeze(1).to_broadcast([16, 8, T // 4]),
+        )
+        w_raw = {(0, 0): load_weight_half(w1, 0, "w_raw00", shared, offset=0)}
+        xw_win = load_words(x_words, T, "xw_win", keep)
+        w_raw[0, 1] = load_weight_half(w1, 1, "w_raw01", keep)
         k1_t = load_list(k1, "k1_t")
         n2_t = load_list(n2, "n2_t")
         n1_t = load_list(n1, "n1_t")
-        w_raw[0, 1] = load_weight_half(w1, 1, "w_raw01")
-        w_raw[1, 0] = load_weight_half(w2, 0, "w_raw10")
-        w_raw[1, 1] = load_weight_half(w2, 1, "w_raw11")
         n3_t = load_list(n3, "n3_t")
+        w_raw[1, 0] = load_weight_half(w2, 0, "w_raw10", keep)
+        w_raw[1, 1] = load_weight_half(w2, 1, "w_raw11", keep)
         n4_t = load_list(n4, "n4_t")
-        ds_win = load_scales(nc.gpsimd, d_scales, G, "ds_win")
-        gs_t = keep.tile([P, PACK], F32, name="gs_t")
-        nc.gpsimd.dma_start(gs_t[:], gs.rearrange("(p t) o -> p (t o)", t=PACK))
+        ds_win = keep.tile([P, G], U8, name="ds_win", align_bytes=64)
+        nc.gpsimd.memset(ds_win[:].bitcast(I32), 0)
+        nc.gpsimd.dma_start(ds_win[0:P:8, :].bitcast(I32), d_scales[0].bitcast(I32))
 
         x_plane = keep.tile([P, 2 * S], U8, name="x_plane", align_bytes=64)
         d_plane = keep.tile([P, H], U8, name="d_plane", align_bytes=64)
@@ -98,10 +96,9 @@ def tile_picked_thqratiorelay_none_p_kernel(
             for half in range(2):
                 dst = grouped[:, :, half * 64 : (half + 1) * 64, :].rearrange("p t m j -> p m j t")
                 src = w_raw[i, half][:].rearrange("p j (m t) -> p m j t", t=PACK)
-                if (i, half) == (1, 1):
-                    nc.vector.tensor_copy(dst, src)
-                else:
-                    nc.scalar.copy(dst, src)
+                nc.scalar.copy(dst, src)
+                if (i, half) == (0, 0):
+                    dw_win = load_words(d_words, G, "dw_win", shared, offset=0)
             codes = keep.tile([P, H], U32, name="w_codes%d" % i, align_bytes=64)
             scales = keep.tile([P, H], U8, name="w_scales%d" % i, align_bytes=64)
             flat = grouped[:].rearrange("p t m j -> p (t m j)")
@@ -116,122 +113,161 @@ def tile_picked_thqratiorelay_none_p_kernel(
 
         y_banks = []
         for t in range(PACK):
-            bank = psum.tile([P, S], F32, name="bank%d" % t)
+            acc = psum.tile([P, S], F32, name="bank%d" % t)
             cols = slice(t * P, (t + 1) * P)
-            for i in (1, 0):
+            passes = (0, 1) if t == 0 else (1, 0)
+            for i in passes:
                 nc.tensor.matmul_mx(
-                    out=bank[:],
+                    out=acc[:],
                     lhsT=w_codes[i][:, cols].bitcast(FP8X4),
                     lhsT_scale=w_scales[i][:, cols],
                     rhs=xw_picked[i][:].bitcast(FP8X4),
                     rhs_scale=x_plane[:, i * S : (i + 1) * S],
-                    start=(i == 1),
-                    stop=(i == 0),
+                    start=(i == passes[0]),
+                    stop=(i == passes[1]),
                 )
-            y_banks.append(bank)
+            y_banks.append(acc)
 
-        ds_picked = keep.tile([P, H], U8, name="ds_picked", tag="w_grouped1", align_bytes=64)
+        ds_picked = keep.tile([P, H], U8, name="ds_picked", tag="w_grouped0", align_bytes=64)
         nc.vector.tensor_copy(ds_picked[:], ds_win[:].indirect(k1_t[:]))
         ds_dealt = keep.tile([P, H], U8, name="ds_dealt", align_bytes=64)
         nc.vector.tensor_copy(
-            ds_dealt[:].rearrange("p (t m) -> p m t", t=PACK),
-            ds_picked[:].rearrange("p (m t) -> p m t", t=PACK),
+            ds_dealt[:].bitcast(I32).rearrange("p (t r q) -> p t r q", t=PACK, r=16),
+            ds_picked[:].bitcast(I32).rearrange("p (r t q) -> p t r q", t=PACK, r=16),
         )
         place_rows(nc.sync, d_plane, ds_dealt)
 
-        dw_win = load_words(d_words, G, "dw_win", tag="w_raw00")
         dw_picked = keep.tile([P, H], U32, name="dw_picked", align_bytes=64)
         nc.vector.tensor_copy(dw_picked[:], dw_win[:].bitcast(U32).indirect(k1_t[:]))
         dw_dealt = keep.tile([P, H], U32, name="dw_dealt", align_bytes=64)
-        nc.vector.tensor_copy(
-            dw_dealt[:].rearrange("p (t m) -> p m t", t=PACK),
-            dw_picked[:].rearrange("p (m t) -> p m t", t=PACK),
-        )
+        for t in range(PACK):
+            nc.sync.dma_start(
+                dw_dealt[:].bitcast(I32).rearrange("p (t r q) -> p t r q", t=PACK, r=16)[:, t],
+                dw_picked[:].bitcast(I32).rearrange("p (r t q) -> p t r q", t=PACK, r=16)[:, t],
+            )
+        gs_t = keep.tile([P, PACK], F32, name="gs_t", tag="w_raw01", align_bytes=64)
+        nc.sync.dma_start(gs_t[:], gs.rearrange("(p t) o -> p (t o)", t=PACK))
 
         def weigh_and_round(t, dt_t):
             for c, (lo, hi) in enumerate(Z_CHUNKS):
                 src = dt_t[:, lo:hi]
-                if c == 0 and t >= 2:
-                    nc.vector.tensor_scalar(
-                        z_grouped[c][:, :, t], src, gs_t[:, t : t + 1], None, ALU.mult
-                    )
-                else:
-                    nc.scalar.activation(
-                        z_grouped[c][:, :, t], src, ACT.Copy, scale=gs_t[:, t : t + 1]
-                    )
+                nc.scalar.activation(
+                    z_grouped[c][:, :, t], src, ACT.Copy, scale=gs_t[:, t : t + 1]
+                )
 
-        dts = []
-        for t in range(PACK):
-            y_t = keep.tile([P, S], F32, name="y%d" % t, align_bytes=64)
-            nc.scalar.copy(y_t[:], y_banks[t][:])
-            pa = keep.tile([P, W], F32, name="pa%d" % t)
-            pb = keep.tile([P, W], F32, name="pb%d" % t)
-            nc.scalar.activation(pb[:], y_t[:].indirect(n2_t[:]), ACT.Copy)
-            nc.scalar.activation(pa[:], y_t[:].indirect(n1_t[:]), ACT.Copy)
-            rb = keep.tile([P, W], F32, name="rb%d" % t)
-            nc.vector.tensor_tensor(rb[:], pa[:], pb[:], ALU.max)
-            dt_t = keep.tile([P, S], F32, name="dt%d" % t)
-            nc.vector.tensor_copy(dt_t[:].indirect(n2_t[:]), rb[:])
-            size = keep.tile([P, W], F32, name="size%d" % t, align_bytes=64)
-            nc.scalar.activation(size[:], pb[:], ACT.Abs)
-            root = keep.tile([P, W], F32, name="root%d" % t, align_bytes=64)
-            nc.scalar.activation(root[:], size[:], ACT.Abs_reciprocal_sqrt, bias=0.5)
-            inv = keep.tile([P, W], F32, name="inv%d" % t)
-            nc.scalar.activation(inv[:], root[:], ACT.Square)
-            nc.vector.tensor_tensor(dt_t[:].indirect(n1_t[:]), pa[:], inv[:], ALU.mult)
-            dts.append(dt_t)
+        def narrow(name, t):
+            if t == 0 and name in HELD:
+                return shared.tile([P, W], F32, name=name + "0", align_bytes=64, offset=1024 * HELD.index(name))
+            return keep.tile([P, W], F32, name="%s%d" % (name, t), align_bytes=64)
+
+        ys = [keep.tile([P, S], F32, name="y0", align_bytes=64)] + [
+            shared.tile([P, S], F32, name="y%d" % t, align_bytes=64, offset=2048 * t) for t in range(1, PACK)
+        ]
+        dts = [keep.tile([P, S], F32, name="dt%d" % t) for t in range(PACK)]
+        pa, pb, rb, size, root, inv = (
+            [narrow(name, t) for t in range(PACK)]
+            for name in ("pa", "pb", "rb", "size", "root", "inv")
+        )
+
+        def fetch(engine, dst, window, offsets):
+            if engine is nc.vector:
+                nc.vector.tensor_copy(dst, window[:].indirect(offsets))
+            else:
+                nc.scalar.activation(dst, window[:].indirect(offsets), ACT.Copy)
+
+        for t in range(PACK + 1):
+            new, old = t < PACK, t >= 1
+            if new:
+                nc.scalar.copy(ys[t][:], y_banks[t][:])
+            if old:
+                nc.scalar.activation(size[t - 1][:], pb[t - 1][:], ACT.Abs)
+            if new:
+                fetch(nc.scalar, pb[t][:], ys[t], n2_t[:])
+            if old:
+                nc.scalar.activation(root[t - 1][:], size[t - 1][:], ACT.Abs_reciprocal_sqrt, bias=0.5)
+            if new:
+                fetch(nc.vector if t == 0 else nc.scalar, pa[t][:], ys[t], n1_t[:])
+                nc.vector.tensor_tensor(rb[t][:], pa[t][:], pb[t][:], ALU.max)
+            if old:
+                nc.scalar.activation(inv[t - 1][:], root[t - 1][:], ACT.Square)
+                nc.vector.tensor_tensor(
+                    dts[t - 1][:].indirect(n1_t[:]), pa[t - 1][:], inv[t - 1][:], ALU.mult
+                )
+            if new:
+                nc.vector.tensor_copy(dts[t][:].indirect(n2_t[:]), rb[t][:])
+
         z_grouped = [
-            keep.tile([P, hi - lo, PACK], BF16, name="z_grouped%d" % lo, tag=tag + str(PACK - 2), align_bytes=64)
-            for (lo, hi), tag in zip(Z_CHUNKS, ("y", "size", "root"))
+            keep.tile([P, hi - lo, PACK], BF16, name="z_grouped%d" % lo, tag=tag, align_bytes=64)
+            for (lo, hi), tag in zip(Z_CHUNKS, ("root2", "size3", "root3"))
         ]
         for t in range(PACK):
             weigh_and_round(t, dts[t])
 
-        z_codes = keep.tile([P, S], U32, name="z_codes", align_bytes=64)
-        z_scales = keep.tile([P, S], U8, name="z_scales", align_bytes=64)
-        for c, (lo, hi) in enumerate(Z_CHUNKS):
+        def quantise_z(c, tag):
+            lo, hi = Z_CHUNKS[c]
+            codes = keep.tile([P, hi - lo], U32, name="z_codes%d" % c, align_bytes=64)
+            scales = keep.tile([P, hi - lo], U8, name="z_scales%d" % c, tag=tag, align_bytes=64)
             nc.vector.quantize_mx(
-                out=z_codes[:, lo:hi].bitcast(FP8X4),
-                scales=z_scales[:, lo:hi],
+                out=codes[:].bitcast(FP8X4),
+                scales=scales[:],
                 in_=z_grouped[c][:].rearrange("p n t -> p (n t)"),
             )
+            return codes, scales
 
         hs = [keep.tile([P, S], F32, name="h%d" % t) for t in range(PACK)]
         sent = [keep.tile([P, S], F32, name="sent%d" % t) for t in range(PACK)]
-        out_rows = out.rearrange("(p t) n -> t p n", t=PACK)
+        out_rows = out.rearrange("(r t q) n -> t r q n", t=PACK, r=16)
 
-        def product_and_send(step, t, lo, hi):
-            bank = psum.tile([P, S], F32, name="bank%d" % ((step + PACK) % 8))
+        def product(dst, t, z):
             cols = slice(t * P, (t + 1) * P)
             nc.tensor.matmul_mx(
-                out=bank[:, : hi - lo],
+                out=dst,
                 lhsT=dw_dealt[:, cols].bitcast(FP8X4),
                 lhsT_scale=d_plane[:, cols],
-                rhs=z_codes[:, lo:hi].bitcast(FP8X4),
-                rhs_scale=z_scales[:, lo:hi],
+                rhs=z[0][:].bitcast(FP8X4),
+                rhs_scale=z[1][:],
                 start=True,
                 stop=True,
             )
+
+        def send(t, lo, hi, sums):
             part = hs[t][:, lo:hi]
-            if step == 0:
-                nc.vector.tensor_scalar(part, bank[:, : hi - lo], 0.0625, None, ALU.mult)
+            if (t, lo) == (0, 0):
+                nc.vector.tensor_scalar(part, sums, 0.0625, None, ALU.mult)
             else:
-                nc.scalar.activation(part, bank[:, : hi - lo], ACT.Copy, scale=0.0625)
+                nc.scalar.activation(part, sums, ACT.Copy, scale=0.0625)
             nc.vector.tensor_copy(sent[t][:].indirect(n3_t[:, lo // 16 : hi // 16]), part)
 
-        def fetch_and_store(t):
-            for c in range(2):
-                cols = slice(c * HALF, (c + 1) * HALF)
-                back = keep.tile([P, HALF], F32, name="back%d%d" % (t, c))
-                looked_up = sent[t][:].indirect(n4_t[:, c * 16 : (c + 1) * 16])
-                nc.scalar.activation(back[:], looked_up, ACT.Copy)
-                res = keep.tile([P, HALF], F32, name="res%d%d" % (t, c))
-                nc.vector.tensor_tensor(res[:], hs[t][:, cols], back[:], ALU.max)
-                nc.sync.dma_start(out_rows[t][:, cols], res[:])
+        def bank(b):
+            return psum.tile([P, S], F32, name="bank%d" % b)
 
-        order = [(0, 0, 128), (1, 0, 128), (0, 128, 256), (1, 128, 256), (0, 256, 512), (2, 0, 256), (1, 256, 512), (3, 0, 256), (2, 256, 512), (3, 256, 512)]
-        for step, (t, lo, hi) in enumerate(order):
-            product_and_send(step, t, lo, hi)
-            if step >= 1 and order[step - 1][2] == S:
-                fetch_and_store(order[step - 1][0])
-        fetch_and_store(PACK - 1)
+        def fetch_and_store(t):
+            back = keep.tile([P, S], F32, name="back%d" % t)
+            res = keep.tile([P, S], F32, name="res%d" % t)
+            for lo in (0, HALF):
+                fetch(nc.scalar, back[:, lo : lo + HALF], sent[t], n4_t[:, lo // 16 : (lo + HALF) // 16])
+            width = HALF if t == PACK - 1 else S
+            for lo in range(0, S, width):
+                cols = slice(lo, lo + width)
+                nc.vector.tensor_tensor(res[:, cols], hs[t][:, cols], back[:, cols], ALU.max)
+                nc.sync.dma_start(out_rows[t][:, :, cols], res[:, cols])
+
+        wide = [bank(6), bank(7)]
+        for c in range(2):
+            lo, hi = Z_CHUNKS[c]
+            z = quantise_z(c, "z_scales%d" % c)
+            for t in range(2):
+                sums = bank((4 + 4 * c + t) % 8)[:, :P]
+                product(sums, t, z)
+                send(t, lo, hi, sums)
+            for t in range(2, PACK):
+                product(wide[t - 2][:, lo:hi], t, z)
+        for t in range(2, PACK):
+            send(t, 0, HALF, wide[t - 2][:, :HALF])
+        z = quantise_z(2, "z_scales1")
+        for t in range(PACK):
+            sums = bank(2 + t)[:, :HALF]
+            product(sums, t, z)
+            send(t, HALF, S, sums)
+        for t in range(PACK):
+            fetch_and_store(t)

@@ -48,6 +48,9 @@ def tile_picked_thqratiorelay_none_p_kernel(
             nc.sync.dma_start(t[:], src.rearrange("(p j) c -> p j c", j=PACK)[:, :, cols])
             return t
 
+        warm = keep.tile([P, 2], F32, name="warm")
+        nc.vector.memset(warm[:, 0:1], 1.0)
+        nc.scalar.activation(warm[:, 1:2], warm[:, 0:1], ACT.Abs_reciprocal_sqrt, bias=0.5)
         offs_t = load_list(offs, "offs_t")
         hz_t = load_list(hz, "hz_t")
         xs_win = keep.tile([P, T], U8, name="xs_win", align_bytes=64)

@@ -43,9 +43,13 @@ def tile_picked_thqratiorelay_none_p_kernel(
             return t
 
         def load_weight_half(src, half, name, pool, **place):
-            t = pool.tile([P, PACK, HALF], F32, name=name, align_bytes=64, **place)
-            cols = slice(half * HALF, (half + 1) * HALF)
-            nc.sync.dma_start(t[:], src.rearrange("(p j) c -> p j c", j=PACK)[:, :, cols])
+            rows = src.rearrange("(p j) c -> p j c", j=PACK)
+            if src is w1:
+                part = rows[:, 2 * half : 2 * half + 2, :]
+            else:
+                part = rows[:, :, half * HALF : (half + 1) * HALF]
+            t = pool.tile(list(part.shape), F32, name=name, align_bytes=64, **place)
+            nc.sync.dma_start(t[:], part)
             return t
 
         warm = keep.tile([P, 2], F32, name="warm")
@@ -97,7 +101,10 @@ def tile_picked_thqratiorelay_none_p_kernel(
         for i in range(2):
             grouped = keep.tile([P, PACK, P, PACK], BF16, name="w_grouped%d" % i, align_bytes=64)
             for half in range(2):
-                dst = grouped[:, :, half * 64 : (half + 1) * 64, :].rearrange("p t m j -> p m j t")
+                if i == 0:
+                    dst = grouped[:, :, :, 2 * half : 2 * half + 2].rearrange("p t m j -> p m j t")
+                else:
+                    dst = grouped[:, :, half * 64 : (half + 1) * 64, :].rearrange("p t m j -> p m j t")
                 src = w_raw[i, half][:].rearrange("p j (m t) -> p m j t", t=PACK)
                 nc.scalar.copy(dst, src)
                 if (i, half) == (0, 0):

from contextlib import ExitStack

import concourse.mybir as mybir

K, T, S, H, W, G = 512, 1024, 512, 512, 256, 2048
FLOPS = 3 * 2 * K * H * S

F32 = mybir.dt.float32
BF16 = mybir.dt.bfloat16
I32 = mybir.dt.int32
U32 = mybir.dt.uint32
U16 = mybir.dt.uint16
U8 = mybir.dt.uint8
FP8X4 = mybir.dt.float8_e4m3fn_x4
ACT = mybir.ActivationFunctionType
ALU = mybir.AluOpType

P = 128
PACK = 4
HALF = 256
HELD = ("pa", "size")
Z_CHUNKS = ((0, 128), (128, 256), (256, 512))


def tile_picked_thqratiorelay_none_p_kernel(
    tc, x_words, x_scales, w1, w2, gs, d_words, d_scales, offs, hz, n1, n2, k1, n3, n4, out
):
    nc = tc.nc
    with ExitStack() as ctx:
        lists = ctx.enter_context(tc.tile_pool(name="lists", bufs=1))
        keep = ctx.enter_context(tc.tile_pool(name="keep", bufs=1))
        shared = ctx.enter_context(tc.tile_pool(name="shared", bufs=1))
        psum = ctx.enter_context(tc.psum_pool(name="psum", bufs=1))

        def load_list(src, name):
            t = lists.tile(list(src.shape), U16, name=name)
            nc.sync.dma_start(t[:], src)
            return t

        def load_words(src, cols, name, pool, **place):
            t = pool.tile([P, cols], I32, name=name, align_bytes=64, **place)
            nc.sync.dma_start(t[:], src[0].rearrange("p c r -> p (c r)").bitcast(I32))
            return t

        def load_weight_half(src, half, name, pool, **place):
            rows = src.rearrange("(p j) c -> p j c", j=PACK)
            if src is w1:
                part = rows[:, 2 * half : 2 * half + 2, :]
            else:
                part = rows[:, :, half * HALF : (half + 1) * HALF]
            t = pool.tile(list(part.shape), F32, name=name, align_bytes=64, **place)
            nc.sync.dma_start(t[:], part)
            return t

        warm = keep.tile([P, 2], F32, name="warm")
        nc.vector.memset(warm[:, 0:1], 1.0)
        nc.scalar.activation(warm[:, 1:2], warm[:, 0:1], ACT.Abs_reciprocal_sqrt, bias=0.5)
        offs_t = load_list(offs, "offs_t")
        hz_t = load_list(hz, "hz_t")
        xs_win = keep.tile([P, T], U8, name="xs_win", align_bytes=64)
        nc.sync.dma_start(
            xs_win[:].bitcast(I32),
            x_scales[0].bitcast(I32).unsqueeze(1).to_broadcast([16, 8, T // 4]),
        )
        w_raw = {(0, 0): load_weight_half(w1, 0, "w_raw00", shared, offset=0)}
        xw_win = load_words(x_words, T, "xw_win", keep)
        w_raw[0, 1] = load_weight_half(w1, 1, "w_raw01", keep)
        k1_t = load_list(k1, "k1_t")
        n2_t = load_list(n2, "n2_t")
        n1_t = load_list(n1, "n1_t")
        n3_t = load_list(n3, "n3_t")
        w_raw[1, 0] = load_weight_half(w2, 0, "w_raw10", keep)
        w_raw[1, 1] = load_weight_half(w2, 1, "w_raw11", keep)
        n4_t = load_list(n4, "n4_t")
        ds_win = keep.tile([P, G], U8, name="ds_win", align_bytes=64)
        nc.gpsimd.memset(ds_win[:].bitcast(I32), 0)
        nc.gpsimd.dma_start(ds_win[0:P:8, :].bitcast(I32), d_scales[0].bitcast(I32))

        x_plane = keep.tile([P, 2 * S], U8, name="x_plane", align_bytes=64)
        d_plane = keep.tile([P, H], U8, name="d_plane", align_bytes=64)
        nc.vector.memset(x_plane[:].bitcast(I32), 0)
        nc.vector.memset(d_plane[:].bitcast(I32), 0)

        def place_rows(queue, plane, picked):
            for j in range(4):
                queue.dma_start(
                    plane[j:P:32, :].bitcast(I32), picked[8 * j : P : 32, :].bitcast(I32)
                )

        xs_picked = keep.tile([P, 2 * S], U8, name="xs_picked", align_bytes=64)
        nc.vector.tensor_copy(xs_picked[:, :S], xs_win[:].indirect(offs_t[:]))
        nc.vector.tensor_copy(xs_picked[:, S:], xs_win[:].indirect(hz_t[:]))
        place_rows(nc.sync, x_plane, xs_picked)
        xw_picked = []
        for i, lst in enumerate((offs_t, hz_t)):
            t = keep.tile([P, S], U32, name="xw_picked%d" % i, align_bytes=64)
            nc.vector.tensor_copy(t[:], xw_win[:].bitcast(U32).indirect(lst[:]))
            xw_picked.append(t)

        w_codes, w_scales = [], []
        for i in range(2):
            grouped = keep.tile([P, PACK, P, PACK], BF16, name="w_grouped%d" % i, align_bytes=64)
            for half in range(2):
                if i == 0:
                    dst = grouped[:, :, :, 2 * half : 2 * half + 2].rearrange("p t m j -> p m j t")
                else:
                    dst = grouped[:, :, half * 64 : (half + 1) * 64, :].rearrange("p t m j -> p m j t")
                src = w_raw[i, half][:].rearrange("p j (m t) -> p m j t", t=PACK)
                nc.scalar.copy(dst, src)
                if (i, half) == (0, 0):
                    dw_win = load_words(d_words, G, "dw_win", shared, offset=0)
            codes = keep.tile([P, H], U32, name="w_codes%d" % i, align_bytes=64)
            scales = keep.tile([P, H], U8, name="w_scales%d" % i, align_bytes=64)
            flat = grouped[:].rearrange("p t m j -> p (t m j)")
            for lo, hi in ((0, H),) if i == 0 else ((0, P), (P, H)):
                nc.vector.quantize_mx(
                    out=codes[:, lo:hi].bitcast(FP8X4),
                    scales=scales[:, lo:hi],
                    in_=flat[:, lo * PACK : hi * PACK],
                )
            w_codes.append(codes)
            w_scales.append(scales)

        y_banks = []
        for t in range(PACK):
            acc = psum.tile([P, S], F32, name="bank%d" % t)
            cols = slice(t * P, (t + 1) * P)
            passes = (0, 1) if t == 0 else (1, 0)
            for i in passes:
                nc.tensor.matmul_mx(
                    out=acc[:],
                    lhsT=w_codes[i][:, cols].bitcast(FP8X4),
                    lhsT_scale=w_scales[i][:, cols],
                    rhs=xw_picked[i][:].bitcast(FP8X4),
                    rhs_scale=x_plane[:, i * S : (i + 1) * S],
                    start=(i == passes[0]),
                    stop=(i == passes[1]),
                )
            y_banks.append(acc)

        ds_picked = keep.tile([P, H], U8, name="ds_picked", tag="w_grouped0", align_bytes=64)
        nc.vector.tensor_copy(ds_picked[:], ds_win[:].indirect(k1_t[:]))
        ds_dealt = keep.tile([P, H], U8, name="ds_dealt", align_bytes=64)
        nc.vector.tensor_copy(
            ds_dealt[:].bitcast(I32).rearrange("p (t r q) -> p t r q", t=PACK, r=16),
            ds_picked[:].bitcast(I32).rearrange("p (r t q) -> p t r q", t=PACK, r=16),
        )
        place_rows(nc.sync, d_plane, ds_dealt)

        dw_picked = keep.tile([P, H], U32, name="dw_picked", align_bytes=64)
        nc.vector.tensor_copy(dw_picked[:], dw_win[:].bitcast(U32).indirect(k1_t[:]))
        dw_dealt = keep.tile([P, H], U32, name="dw_dealt", align_bytes=64)
        for t in range(PACK):
            nc.sync.dma_start(
                dw_dealt[:].bitcast(I32).rearrange("p (t r q) -> p t r q", t=PACK, r=16)[:, t],
                dw_picked[:].bitcast(I32).rearrange("p (r t q) -> p t r q", t=PACK, r=16)[:, t],
            )
        gs_t = keep.tile([P, PACK], F32, name="gs_t", tag="w_raw01", align_bytes=64)
        nc.sync.dma_start(gs_t[:], gs.rearrange("(p t) o -> p (t o)", t=PACK))

        def weigh_and_round(t, dt_t):
            for c, (lo, hi) in enumerate(Z_CHUNKS):
                src = dt_t[:, lo:hi]
                nc.scalar.activation(
                    z_grouped[c][:, :, t], src, ACT.Copy, scale=gs_t[:, t : t + 1]
                )

        def narrow(name, t):
            if t == 0 and name in HELD:
                return shared.tile([P, W], F32, name=name + "0", align_bytes=64, offset=1024 * HELD.index(name))
            return keep.tile([P, W], F32, name="%s%d" % (name, t), align_bytes=64)

        ys = [keep.tile([P, S], F32, name="y0", align_bytes=64)] + [
            shared.tile([P, S], F32, name="y%d" % t, align_bytes=64, offset=2048 * t) for t in range(1, PACK)
        ]
        dts = [keep.tile([P, S], F32, name="dt%d" % t) for t in range(PACK)]
        pa, pb, rb, size, root, inv = (
            [narrow(name, t) for t in range(PACK)]
            for name in ("pa", "pb", "rb", "size", "root", "inv")
        )

        def fetch(engine, dst, window, offsets):
            if engine is nc.vector:
                nc.vector.tensor_copy(dst, window[:].indirect(offsets))
            else:
                nc.scalar.activation(dst, window[:].indirect(offsets), ACT.Copy)

        for t in range(PACK + 1):
            new, old = t < PACK, t >= 1
            if new:
                nc.scalar.copy(ys[t][:], y_banks[t][:])
            if old:
                nc.scalar.activation(size[t - 1][:], pb[t - 1][:], ACT.Abs)
            if new:
                fetch(nc.scalar, pb[t][:], ys[t], n2_t[:])
            if old:
                nc.scalar.activation(root[t - 1][:], size[t - 1][:], ACT.Abs_reciprocal_sqrt, bias=0.5)
            if new:
                fetch(nc.vector if t == 0 else nc.scalar, pa[t][:], ys[t], n1_t[:])
                nc.vector.tensor_tensor(rb[t][:], pa[t][:], pb[t][:], ALU.max)
            if old:
                nc.scalar.activation(inv[t - 1][:], root[t - 1][:], ACT.Square)
                nc.vector.tensor_tensor(
                    dts[t - 1][:].indirect(n1_t[:]), pa[t - 1][:], inv[t - 1][:], ALU.mult
                )
            if new:
                nc.vector.tensor_copy(dts[t][:].indirect(n2_t[:]), rb[t][:])

        z_grouped = [
            keep.tile([P, hi - lo, PACK], BF16, name="z_grouped%d" % lo, tag=tag, align_bytes=64)
            for (lo, hi), tag in zip(Z_CHUNKS, ("root2", "size3", "root3"))
        ]
        for t in range(PACK):
            weigh_and_round(t, dts[t])

        def quantise_z(c, tag):
            lo, hi = Z_CHUNKS[c]
            codes = keep.tile([P, hi - lo], U32, name="z_codes%d" % c, align_bytes=64)
            scales = keep.tile([P, hi - lo], U8, name="z_scales%d" % c, tag=tag, align_bytes=64)
            nc.vector.quantize_mx(
                out=codes[:].bitcast(FP8X4),
                scales=scales[:],
                in_=z_grouped[c][:].rearrange("p n t -> p (n t)"),
            )
            return codes, scales

        hs = [keep.tile([P, S], F32, name="h%d" % t) for t in range(PACK)]
        sent = [keep.tile([P, S], F32, name="sent%d" % t) for t in range(PACK)]
        out_rows = out.rearrange("(r t q) n -> t r q n", t=PACK, r=16)

        def product(dst, t, z):
            cols = slice(t * P, (t + 1) * P)
            nc.tensor.matmul_mx(
                out=dst,
                lhsT=dw_dealt[:, cols].bitcast(FP8X4),
                lhsT_scale=d_plane[:, cols],
                rhs=z[0][:].bitcast(FP8X4),
                rhs_scale=z[1][:],
                start=True,
                stop=True,
            )

        def send(t, lo, hi, sums):
            part = hs[t][:, lo:hi]
            if (t, lo) == (0, 0):
                nc.vector.tensor_scalar(part, sums, 0.0625, None, ALU.mult)
            else:
                nc.scalar.activation(part, sums, ACT.Copy, scale=0.0625)
            nc.vector.tensor_copy(sent[t][:].indirect(n3_t[:, lo // 16 : hi // 16]), part)

        def bank(b):
            return psum.tile([P, S], F32, name="bank%d" % b)

        def fetch_and_store(t):
            back = keep.tile([P, S], F32, name="back%d" % t)
            res = keep.tile([P, S], F32, name="res%d" % t)
            for lo in (0, HALF):
                fetch(nc.scalar, back[:, lo : lo + HALF], sent[t], n4_t[:, lo // 16 : (lo + HALF) // 16])
            width = HALF if t == PACK - 1 else S
            for lo in range(0, S, width):
                cols = slice(lo, lo + width)
                nc.vector.tensor_tensor(res[:, cols], hs[t][:, cols], back[:, cols], ALU.max)
                nc.sync.dma_start(out_rows[t][:, :, cols], res[:, cols])

        wide = [bank(6), bank(7)]
        for c in range(2):
            lo, hi = Z_CHUNKS[c]
            z = quantise_z(c, "z_scales%d" % c)
            for t in range(2):
                sums = bank((4 + 4 * c + t) % 8)[:, :P]
                product(sums, t, z)
                send(t, lo, hi, sums)
            for t in range(2, PACK):
                product(wide[t - 2][:, lo:hi], t, z)
        for t in range(2, PACK):
            send(t, 0, HALF, wide[t - 2][:, :HALF])
        z = quantise_z(2, "z_scales1")
        for t in range(PACK):
            sums = bank(2 + t)[:, :HALF]
            product(sums, t, z)
            send(t, HALF, S, sums)
        for t in range(PACK):
            fetch_and_store(t)
